import numpy as np, ml_dtypes
CORES = [3,7,11,15,131,135,139,143]
N = 8
import mx_ref
BF = ml_dtypes.bfloat16
def entries(a):
    return np.ascontiguousarray(a.T).reshape(-1)
def table(e):
    return np.ascontiguousarray(np.reshape(e, (-1, 16)).T).astype(np.int32)
def cols(t, e):
    v = np.concatenate([t.reshape(128, -1, 4), np.zeros((128, 1, 4), BF)], axis=1)
    return np.ascontiguousarray(v[:, e]).reshape(128, -1)
def pick(q, e):
    c = np.concatenate([q[0].reshape(128, -1, 4), np.zeros((128, 1, 4), np.uint8)], axis=1); s = np.concatenate([q[1], np.ones((16, 1), np.uint8)], axis=1)
    return (np.ascontiguousarray(c[:, e].reshape(128, -1)), np.ascontiguousarray(s[:, e]))
def join(*qs):
    return (np.concatenate([q[0] for q in qs], axis=1), np.concatenate([q[1] for q in qs], axis=1))
def put(q, e, v):
    c, s = q[0].reshape(128, -1, 4).copy(), q[1].copy(); c[:, e] = v[0].reshape(128, -1, 4); s[:, e] = v[1]
    return (c.reshape(128, -1), s)
def pk(c, s):
    return (np.ascontiguousarray(c), mx_ref.live(s))
def emit(q):
    return q[0], q[1]
def decode(q):
    o = []
    for b in range(4):
        e = np.zeros((128, 128, 4), np.float32); e[np.arange(128), np.arange(128), b] = 1
        o.append(mx_ref.matmul(mx_ref.quantize(e.reshape(128, 512).astype(BF)), q))
    return np.stack(o, axis=2).reshape(128, -1)
def f(rng, *shape):
    return mx_ref.flush((rng.standard_normal(shape, dtype=np.float32) * np.exp2(rng.integers(-2, 3, shape[:-1] + (1,)))).astype(BF))
def wide(rng, *shape, cols=0):
    v = rng.standard_normal(shape, dtype=np.float32) * np.exp2(rng.integers(-12, 13, shape)).astype(np.float32)
    if cols: v *= np.repeat(np.exp2(rng.integers(-cols, cols + 1, shape[:-2] + (1, shape[-1] // 4))) * (rng.random(shape[:-2] + (1, shape[-1] // 4)) > 0.0625), 4, axis=-1).astype(np.float32)
    return mx_ref.flush(v.astype(BF))
T, CAPP = 128, 64
def lists(rng, count, high=False, among=T, unnamed=0):
    sn, so = np.full((N, N * CAPP), -1), np.zeros((N, 512), int)
    for d in range(N):
        filled = []
        for s in range(N):
            c = np.sort(rng.permutation(CAPP)[:count[s, d]]); k = rng.permutation(among)[:c.size]
            sn[s, d * CAPP + c] = np.sort(k)[::-1] if high else k
            filled.append(s * CAPP + c)
        filled = np.concatenate(filled)
        if unnamed: filled = rng.permutation(filled)[unnamed:]
        o = np.concatenate([filled, rng.choice(filled, 512 - filled.size)])
        so[d] = np.sort(o)[::-1] if high else rng.permutation(o)
    return {"sn": np.stack([table(v) for v in sn]), "so": np.stack([table(v) for v in so])}
def setup_inputs(rng):
    return {"x": f(rng, N, 128, 4 * T), **lists(rng, rng.integers(1, CAPP + 1, (N, N)))}
def setup_inputs_full(rng):
    return {**setup_inputs(rng), **lists(rng, np.full((N, N), CAPP))}
def setup_inputs_one(rng):
    n = np.zeros((N, N), int); n[rng.integers(0, N)] = 3
    return {**setup_inputs(rng), **lists(rng, n, among=rng.permutation(T)[:3])}
def setup_inputs_own(rng):
    return {**setup_inputs(rng), **lists(rng, CAPP * np.eye(N, dtype=int))}
def setup_inputs_reversed(rng):
    return {**setup_inputs(rng), **lists(rng, rng.integers(1, CAPP + 1, (N, N)), high=True, unnamed=3)}
def setup_inputs_spread(rng):
    d = setup_inputs(rng); d["x"] = wide(rng, N, 128, 4 * T, cols=8); return d
def check_inputs(d):
    b = []
    a = np.stack([entries(d["sn"][s]) for s in range(N)])
    for r in range(N):
        pairs = [a[r, q * CAPP:q * CAPP + CAPP] for q in range(N)]
        if a[r].min() < -1 or a[r].max() >= T or any(len(set(g[g >= 0].tolist())) != (g >= 0).sum() for g in pairs): b.append("sn")
        e = entries(d["so"][r])
        if e.min() < 0 or e.max() >= N * CAPP: b.append("so")
        elif (a[e // CAPP, r * CAPP + e % CAPP] < 0).any(): b.append("so")
    return b
def reference(x, sn, so):
    v = np.concatenate([x[s] for s in range(N)], axis=1)
    a = np.stack([entries(sn[s]) for s in range(N)])
    fc, fs = np.zeros((N, 128, 2048), np.uint8), np.zeros((N, 16, 512), np.uint8)
    bc, bs = np.zeros((N, 128, 2048), np.uint8), np.zeros((N, 16, 512), np.uint8)
    for d in range(N):
        e = entries(so[d]); s = e // CAPP
        F = mx_ref.quantize(cols(v, s * T + a[s, d * CAPP + e % CAPP]))
        fc[d], fs[d] = emit(F)
        m = decode(F).reshape(128, 512, 4).transpose(0, 2, 1).reshape(512, 512)
        m = np.ascontiguousarray(m.T).astype(BF)
        bt = []
        for b in range(4):
            k = np.ascontiguousarray(m[:, 128 * b:128 * b + 128]).reshape(128, 4, 128)
            bt.append(mx_ref.quantize(np.ascontiguousarray(k.transpose(0, 2, 1)).reshape(128, 512)))
        bc[d], bs[d] = emit(join(*bt))
    return {"fc": fc, "fs": fs, "bc": bc, "bs": bs}

@@ -1,0 +1,226 @@
+from concourse.bass import DstId, RemoteDMATransfer
+from concourse.mybir import dt, AluOpType, ActivationFunctionType
+
+CAPP = 64
+COPY = ActivationFunctionType.Copy
+PARTS = [(0, 384), (384, 512)]
+ON_VECTOR = [(0, 3)]
+
+SCRATCH = {
+    "xt": ("sbuf", [128, 512], "bfloat16"),
+    "xq": ("sbuf", [128, 128], "float8_e4m3fn_x4"),
+    "xp": ("sbuf", [128, 128], "uint8"),
+    "snl": ("sbuf", [128, 32], "int32"),
+    "sno": ("sbuf", [128, 32], "uint16"),
+    "sol": ("sbuf", [128, 132], "int32"),
+    "soo": ("sbuf", [128, 32], "uint16"),
+    "pidx": ("sbuf", [128, 32], "int32"),
+    "kidx": ("sbuf", [128, 32], "int32"),
+    "plow": ("sbuf", [128, 32], "int32"),
+    "phigh": ("sbuf", [128, 32], "int32"),
+    "isum": ("sbuf", [128, 32], "int32"),
+    "isum2": ("sbuf", [128, 32], "int32"),
+    "plow2": ("sbuf", [128, 32], "int32"),
+    "inv": ("sbuf", [128, 32], "uint16"),
+    "ones": ("sbuf", [128, 128], "bfloat16"),
+    "eye": ("sbuf", [128, 128], "bfloat16"),
+    "idt": ("sbuf", [128, 2048], "bfloat16"),
+    "idq": ("sbuf", [128, 512], "float8_e4m3fn_x4"),
+    "idp": ("sbuf", [128, 512], "uint8"),
+    "slq": ("sbuf", [128, 512], "float8_e4m3fn_x4"),
+    "slp": ("sbuf", [128, 512], "uint8"),
+    "ldq": ("sbuf", [128, 512], "float8_e4m3fn_x4"),
+    "ldp": ("sbuf", [128, 512], "uint8"),
+    "gq": ("sbuf", [128, 512], "float8_e4m3fn_x4"),
+    "gp": ("sbuf", [128, 512], "uint8"),
+    "fq": ("sbuf", [128, 512], "float8_e4m3fn_x4"),
+    "fp": ("sbuf", [128, 512], "uint8"),
+    "bt": ("sbuf", [128, 2048], "bfloat16"),
+    "bq": ("sbuf", [128, 512], "float8_e4m3fn_x4"),
+    "bp": ("sbuf", [128, 512], "uint8"),
+    "acc": ("psum", [128, 4096], "float32"),
+}
+SEMAPHORES = (["ldx", "ldsa", "ldsb", "ldo", "ldo2", "one", "zero", "eyed", "iop", "iok", "low", "high", "low2", "su", "su2", "invd",
+               "idd", "idqd", "snd", "sod", "xqd", "vown", "sown", "fqd", "fpd", "arrc", "arrp", "sent", "std", "std2"]
+              + ["%s%d" % (a, k) for a in ("vp", "sp", "gqd", "gpd") for k in range(4)]
+              + ["mm%d" % k for k in range(8)] + ["cp%d" % k for k in range(8)] + ["bqd0", "bqd1"])
+
+
+def plan(r, cores, topo):
+    me = cores[r]
+    home = [q for q in range(len(cores)) if cores[q] in topo.cores_of(me)]
+    groups = []
+    for q in range(len(cores)):
+        if q not in home and not any(q in k for k in groups):
+            groups.append([w for w in range(len(cores)) if cores[w] in topo.cores_of(cores[q])])
+
+    def near(k):
+        return 1 if topo.mates(me, cores[k[0]]) else 2 if topo.same_plane(me, cores[k[0]]) else 0
+    groups.sort(key=near)
+    off = topo.engines(me, cores[groups[0][0]])
+    spare = [e for e in topo.engines(me, [c for c in topo.cores_of(me) if c != me][0]) if e not in off]
+
+    def deal(ranks):
+        w = 1
+        while 2 * w * len(ranks) <= len(off):
+            w *= 2
+        return [(d, off[w * i:w * i + w]) for i, d in enumerate(ranks)]
+    calls = [deal(groups[0]), deal(groups[1] + groups[2])]
+    sib = [q for q in home if q != r][0]
+    calls[1] = calls[1] + [(sib, spare[:2])]
+    return groups, sib, calls
+
+
+def rank_program(g, core, T, topo):
+    r = T.rank_of(core)
+    if r is None:
+        return
+    S = T.sem
+    v, s, y, te = g.vector, g.scalar, g.sync, g.tensor
+    groups, sib, calls = plan(r, T.cores, topo)
+    due = 0
+    for q in range(len(T.cores)):
+        if q != r:
+            for call in plan(q, T.cores, topo)[2]:
+                due += sum(len(e) for d, e in call if d == r)
+
+    def u32(t, a, b):
+        return t[:, a:b].bitcast(dt.uint32)
+
+    def u8(t, a, b):
+        return t[:, a:b].bitcast(dt.uint8)
+
+    y.dma_start(T.xt[:], T.x[:]).then_inc(S.ldx, 16)
+    for k in range(3):
+        y.dma_start(T.snl[16 * k:16 * k + 16, :], T.sn[:]).then_inc(S.ldsa, 16)
+    for k in range(3, 8):
+        s.dma_start(T.snl[16 * k:16 * k + 16, :], T.sn[:]).then_inc(S.ldsb, 16)
+    for k in range(2):
+        for u in range(4):
+            a = 16 * k + 4 * u
+            y.dma_start(T.sol[a:a + 4, 3 - u:131 - u], T.so[:]).then_inc(S.ldo, 16)
+    y.wait_ge(S.ldo, 128)
+    for k in range(1, 4):
+        y.dma_start(T.sol[32 * k:32 * k + 32, 3:128], T.sol[0:32, 3:128]).then_inc(S.ldo2, 16)
+
+    g.iota(T.pidx[:], [[0, 32]], 0, 1).then_inc(S.iop, 1)
+    g.iota(T.kidx[:], [[4, 32]], 0, 0).then_inc(S.iok, 1)
+    g.wait_ge(S.one, 1)
+    g.affine_select(T.eye[:], T.ones[:], [[-1, 128]], AluOpType.is_equal, 0.0, 0, 1).then_inc(S.eyed, 1)
+
+    v.memset(T.ones[:], 1.0).then_inc(S.one, 1)
+    v.memset(T.idt[:], 0.0).then_inc(S.zero, 1)
+    v.wait_ge(S.zero, 1)
+    v.wait_ge(S.eyed, 1)
+    for t in range(4):
+        v.tensor_copy(T.idt[:, 5 * t:2048:16], T.eye[:]).then_inc(S.idd, 1)
+
+    v.wait_ge(S.ldx, 16)
+    v.quantize_mx(T.xq[:], T.xp[:], T.xt[:]).then_inc(S.xqd, 1)
+    v.wait_ge(S.ldsa, 48)
+    v.wait_ge(S.ldsb, 80)
+    v.tensor_copy(T.sno[:], T.snl[:]).then_inc(S.snd, 1)
+    picks = [(k[0], len(k)) for k in groups] + [(sib, 1)]
+    v.wait_ge(S.xqd, 1)
+    v.wait_ge(S.snd, 1)
+    s.wait_ge(S.xqd, 1)
+    s.wait_ge(S.snd, 1)
+    for i, (d, n) in enumerate(picks):
+        a, b, o = CAPP * d, CAPP * (d + n), T.sno[:, 4 * d:4 * (d + n)]
+        v.tensor_copy(u32(T.slq, a, b), u32(T.xq, 0, 128).indirect(o)).then_inc(S["vp%d" % i], 1)
+        s.activation(T.slp[:, a:b], T.xp[:, 0:128].indirect(o), COPY).then_inc(S["sp%d" % i], 1)
+    a, b, o = CAPP * r, CAPP * (r + 1), T.sno[:, 4 * r:4 * r + 4]
+    v.tensor_copy(u32(T.ldq, a, b), u32(T.xq, 0, 128).indirect(o)).then_inc(S.vown, 1)
+    s.activation(T.ldp[:, a:b], T.xp[:, 0:128].indirect(o), COPY).then_inc(S.sown, 1)
+
+    needs = [[0], [1, 2, 3]]
+    nsent = 0
+    for i, codes in ((0, True), (0, False), (1, False), (1, True)):
+        for k in needs[i]:
+            g.wait_ge(S["%s%d" % ("vp" if codes else "sp", k)], 1)
+        tr = []
+        for d, eng in calls[i]:
+            rid, pid = topo.addr(T.cores[d], core)
+            a, c = CAPP * d, CAPP * r
+            src = u8(T.slq, a, a + CAPP) if codes else T.slp[:, a:a + CAPP]
+            dst = u8(T.ldq, c, c + CAPP) if codes else T.ldp[:, c:c + CAPP]
+            tr.append(RemoteDMATransfer(dst_ids=[DstId(rid=rid, pnc=pid)], dma_engine_mask=sum(1 << e for e in eng),
+                                        remote_sem=S.arrc if codes else S.arrp, src=src, dst=dst))
+            nsent += len(eng)
+        g.remote_dma_fused(tr, local_sem=S.sent)
+
+    v.wait_ge(S.idd, 4)
+    v.quantize_mx(T.idq[:], T.idp[:], T.idt[:]).then_inc(S.idqd, 1)
+    v.wait_ge(S.iop, 1)
+    v.tensor_scalar(T.plow[:], T.pidx[:], 3, None, AluOpType.bitwise_and).then_inc(S.low, 1)
+    v.tensor_scalar(T.phigh[:], T.pidx[:], 15, 2, AluOpType.bitwise_and, AluOpType.arith_shift_right).then_inc(S.high, 1)
+    v.wait_ge(S.low, 1)
+    v.tensor_scalar(T.plow2[:], T.plow[:], 128, None, AluOpType.mult).then_inc(S.low2, 1)
+    v.wait_ge(S.iok, 1)
+    v.wait_ge(S.high, 1)
+    v.tensor_tensor(T.isum[:], T.phigh[:], T.kidx[:], AluOpType.add).then_inc(S.su, 1)
+    v.wait_ge(S.su, 1)
+    v.wait_ge(S.low2, 1)
+    v.tensor_tensor(T.isum2[:], T.isum[:], T.plow2[:], AluOpType.add).then_inc(S.su2, 1)
+    v.wait_ge(S.su2, 1)
+    v.tensor_copy(T.inv[:], T.isum2[:]).then_inc(S.invd, 1)
+    v.wait_ge(S.ldo2, 48)
+    v.tensor_copy(T.soo[:], T.sol[:, 3:131:4]).then_inc(S.sod, 1)
+
+    v.wait_ge(S.sod, 1)
+    v.wait_ge(S.vown, 1)
+    v.wait_ge(S.arrc, due)
+    s.wait_ge(S.sod, 1)
+    s.wait_ge(S.sown, 1)
+    s.wait_ge(S.invd, 1)
+    s.wait_ge(S.arrp, due)
+    for t in range(4):
+        a, b, o = 128 * t, 128 * t + 128, T.soo[:, 8 * t:8 * t + 8]
+        v.tensor_copy(u32(T.gq, a, b), u32(T.ldq, 0, 512).indirect(o)).then_inc(S["gqd%d" % t], 1)
+        s.activation(T.gp[:, a:b], T.ldp[:, 0:512].indirect(o), COPY).then_inc(S["gpd%d" % t], 1)
+    for t in range(4):
+        v.wait_ge(S["gqd%d" % t], 1)
+        s.wait_ge(S["gpd%d" % t], 1)
+    v.wait_ge(S.invd, 1)
+    v.tensor_copy(u32(T.fq, 0, 512), u32(T.gq, 0, 512).indirect(T.inv[:, 0:32])).then_inc(S.fqd, 1)
+    s.activation(T.fp[:, 0:512], T.gp[:, 0:512].indirect(T.inv[:, 0:32]), COPY).then_inc(S.fpd, 1)
+
+    te.wait_ge(S.idqd, 1)
+    for h, (a, b) in enumerate(PARTS):
+        for t in range(4):
+            if h == 0:
+                te.wait_ge(S["gpd%d" % t], 1)
+                te.wait_ge(S["gqd%d" % t], 1)
+            k = 4 * h + t
+            te.matmul_mx(T.acc[:, 512 * k:512 * k + b - a], T.gq[:, 128 * t:128 * t + 128], T.gp[:, 128 * t:128 * t + 128],
+                         T.idq[:, a:b], T.idp[:, a:b], True, True).then_inc(S["mm%d" % k], 1)
+
+    for h, (a, b) in enumerate(PARTS):
+        for t in range(4):
+            k = 4 * h + t
+            out, src = T.bt[:, 4 * a + t:4 * b:4], T.acc[:, 512 * k:512 * k + b - a]
+            if (h, t) in ON_VECTOR:
+                v.wait_ge(S["mm%d" % k], 1)
+                v.tensor_copy(out, src).then_inc(S["cp%d" % k], 1)
+            else:
+                s.wait_ge(S["mm%d" % k], 1)
+                s.activation(out, src, COPY).then_inc(S["cp%d" % k], 1)
+        for t in range(4):
+            v.wait_ge(S["cp%d" % (4 * h + t)], 1)
+        v.quantize_mx(T.bq[:, a:b], T.bp[:, a:b], T.bt[:, 4 * a:4 * b]).then_inc(S["bqd%d" % h], 1)
+
+    y.wait_ge(S.fpd, 1)
+    for k in range(4):
+        y.dma_start(T.fs[4 * k:4 * k + 4, 0:512], T.fp[32 * k:32 * k + 4, 0:512]).then_inc(S.std, 16)
+    y.wait_ge(S.fqd, 1)
+    y.dma_start(T.fc[:, :], u8(T.fq, 0, 512)).then_inc(S.std, 16)
+    for h, (a, b) in enumerate(PARTS):
+        y.wait_ge(S["bqd%d" % h], 1)
+        y.dma_start(T.bc[:, 4 * a:4 * b], u8(T.bq, a, b)).then_inc(S.std, 16)
+        s.wait_ge(S["bqd%d" % h], 1)
+    for k in range(4):
+        (s if k < 3 else y).dma_start(T.bs[4 * k:4 * k + 4, 0:512], T.bp[32 * k:32 * k + 4, 0:512]).then_inc(
+            S.std2 if k < 3 else S.std, 16)
+    y.wait_ge(S.std, 16 * 8)
+    s.wait_ge(S.std2, 48)
+    g.wait_ge(S.sent, nsent)

@@ -2,9 +2,11 @@ from concourse.bass import DstId, RemoteDMATransfer
 from concourse.mybir import dt, AluOpType, ActivationFunctionType
 
 CAPP = 64
+FRONT, MID, BACK = 1, 2, 10
 COPY = ActivationFunctionType.Copy
 PARTS = [(0, 384), (384, 512)]
 ON_VECTOR = [(0, 3)]
+G_PLANES_ON_VECTOR = [1, 2]
 
 SCRATCH = {
     "xt": ("sbuf", [128, 512], "bfloat16"),
@@ -13,15 +15,13 @@ SCRATCH = {
     "snl": ("sbuf", [128, 32], "int32"),
     "sno": ("sbuf", [128, 32], "uint16"),
     "sol": ("sbuf", [128, 132], "int32"),
-    "soo": ("sbuf", [128, 32], "uint16"),
-    "pidx": ("sbuf", [128, 32], "int32"),
-    "kidx": ("sbuf", [128, 32], "int32"),
-    "plow": ("sbuf", [128, 32], "int32"),
-    "phigh": ("sbuf", [128, 32], "int32"),
-    "isum": ("sbuf", [128, 32], "int32"),
-    "isum2": ("sbuf", [128, 32], "int32"),
-    "plow2": ("sbuf", [128, 32], "int32"),
-    "inv": ("sbuf", [128, 32], "uint16"),
+    "lst": ("sbuf", [128, 64], "int32"),
+    "blk": ("sbuf", [128, 64], "int32"),
+    "mvf": ("sbuf", [128, 64], "int32"),
+    "mvb": ("sbuf", [128, 64], "int32"),
+    "mov": ("sbuf", [128, 64], "int32"),
+    "col": ("sbuf", [128, 64], "int32"),
+    "soo": ("sbuf", [128, 64], "uint16"),
     "ones": ("sbuf", [128, 128], "bfloat16"),
     "eye": ("sbuf", [128, 128], "bfloat16"),
     "idt": ("sbuf", [128, 2048], "bfloat16"),
@@ -29,8 +29,8 @@ SCRATCH = {
     "idp": ("sbuf", [128, 512], "uint8"),
     "slq": ("sbuf", [128, 512], "float8_e4m3fn_x4"),
     "slp": ("sbuf", [128, 512], "uint8"),
-    "ldq": ("sbuf", [128, 512], "float8_e4m3fn_x4"),
-    "ldp": ("sbuf", [128, 512], "uint8"),
+    "ldq": ("sbuf", [128, 768], "float8_e4m3fn_x4"),
+    "ldp": ("sbuf", [128, 768], "uint8"),
     "gq": ("sbuf", [128, 512], "float8_e4m3fn_x4"),
     "gp": ("sbuf", [128, 512], "uint8"),
     "fq": ("sbuf", [128, 512], "float8_e4m3fn_x4"),
@@ -40,9 +40,10 @@ SCRATCH = {
     "bp": ("sbuf", [128, 512], "uint8"),
     "acc": ("psum", [128, 4096], "float32"),
 }
-SEMAPHORES = (["ldx", "ldsa", "ldsb", "ldo", "ldo2", "one", "zero", "eyed", "iop", "iok", "low", "high", "low2", "su", "su2", "invd",
-               "idd", "idqd", "snd", "sod", "xqd", "vown", "sown", "fqd", "fpd", "arrc", "arrp", "sent", "std", "std2"]
-              + ["%s%d" % (a, k) for a in ("vp", "sp", "gqd", "gpd") for k in range(4)]
+SEMAPHORES = (["ldx", "lds", "ldo", "one", "zero", "eyed", "idd", "idqd", "snd", "step", "blkd", "mvd", "movd", "cold", "sod", "xqd",
+               "fqd", "fpd", "arrw", "arrp", "arrc", "sent", "std", "std2"]
+              + ["%s%d" % (a, k) for a in ("vp", "sp") for k in range(5)]
+              + ["%s%d" % (a, k) for a in ("gqd", "gpd") for k in range(4)]
               + ["mm%d" % k for k in range(8)] + ["cp%d" % k for k in range(8)] + ["bqd0", "bqd1"])
 
 
@@ -57,18 +58,18 @@ def plan(r, cores, topo):
     def near(k):
         return 1 if topo.mates(me, cores[k[0]]) else 2 if topo.same_plane(me, cores[k[0]]) else 0
     groups.sort(key=near)
+    peer = [[q for q in k if topo.die(cores[q]) == topo.die(me)][0] for k in groups]
+    other = [[q for q in k if q not in peer][0] for k in groups]
+    ends = peer[:2] if r == home[1] else peer[1::-1]
     off = topo.engines(me, cores[groups[0][0]])
     spare = [e for e in topo.engines(me, [c for c in topo.cores_of(me) if c != me][0]) if e not in off]
+    return {"sib": [q for q in home if q != r][0], "groups": groups, "peer": peer, "other": other, "ends": ends,
+            "off": off, "spare": spare}
 
-    def deal(ranks):
-        w = 1
-        while 2 * w * len(ranks) <= len(off):
-            w *= 2
-        return [(d, off[w * i:w * i + w]) for i, d in enumerate(ranks)]
-    calls = [deal(groups[0]), deal(groups[1] + groups[2])]
-    sib = [q for q in home if q != r][0]
-    calls[1] = calls[1] + [(sib, spare[:2])]
-    return groups, sib, calls
+
+def deal(items, engines):
+    w = len(engines) // len(items)
+    return [(it, engines[w * i:w * i + w]) for i, it in enumerate(items)]
 
 
 def rank_program(g, core, T, topo):
@@ -77,12 +78,15 @@ def rank_program(g, core, T, topo):
         return
     S = T.sem
     v, s, y, te = g.vector, g.scalar, g.sync, g.tensor
-    groups, sib, calls = plan(r, T.cores, topo)
-    due = 0
-    for q in range(len(T.cores)):
-        if q != r:
-            for call in plan(q, T.cores, topo)[2]:
-                due += sum(len(e) for d, e in call if d == r)
+    P = plan(r, T.cores, topo)
+    sib, groups, peer, other, ends, off, spare = [P[k] for k in ("sib", "groups", "peer", "other", "ends", "off", "spare")]
+
+    def place(src, dst):
+        e = plan(dst, T.cores, topo)["ends"]
+        return CAPP * (FRONT if src == e[0] else BACK if src == e[1] else MID + src)
+
+    at = [CAPP * d for d in range(len(T.cores))]
+    at[groups[1][0]], at[groups[1][1]] = at[groups[1][1]], at[groups[1][0]]
 
     def u32(t, a, b):
         return t[:, a:b].bitcast(dt.uint32)
@@ -91,99 +95,124 @@ def rank_program(g, core, T, topo):
         return t[:, a:b].bitcast(dt.uint8)
 
     y.dma_start(T.xt[:], T.x[:]).then_inc(S.ldx, 16)
-    for k in range(3):
-        y.dma_start(T.snl[16 * k:16 * k + 16, :], T.sn[:]).then_inc(S.ldsa, 16)
-    for k in range(3, 8):
-        s.dma_start(T.snl[16 * k:16 * k + 16, :], T.sn[:]).then_inc(S.ldsb, 16)
     for k in range(2):
+        s.dma_start(T.snl[16 * k:16 * k + 16, :], T.sn[:]).then_inc(S.lds, 16)
+    for k in range(2):
+        y.dma_start(T.lst[16 * k:16 * k + 16, 32:64], T.so[:]).then_inc(S.ldo, 16)
         for u in range(4):
             a = 16 * k + 4 * u
             y.dma_start(T.sol[a:a + 4, 3 - u:131 - u], T.so[:]).then_inc(S.ldo, 16)
-    y.wait_ge(S.ldo, 128)
-    for k in range(1, 4):
-        y.dma_start(T.sol[32 * k:32 * k + 32, 3:128], T.sol[0:32, 3:128]).then_inc(S.ldo2, 16)
 
-    g.iota(T.pidx[:], [[0, 32]], 0, 1).then_inc(S.iop, 1)
-    g.iota(T.kidx[:], [[4, 32]], 0, 0).then_inc(S.iok, 1)
     g.wait_ge(S.one, 1)
     g.affine_select(T.eye[:], T.ones[:], [[-1, 128]], AluOpType.is_equal, 0.0, 0, 1).then_inc(S.eyed, 1)
-
     v.memset(T.ones[:], 1.0).then_inc(S.one, 1)
     v.memset(T.idt[:], 0.0).then_inc(S.zero, 1)
-    v.wait_ge(S.zero, 1)
-    v.wait_ge(S.eyed, 1)
-    for t in range(4):
-        v.tensor_copy(T.idt[:, 5 * t:2048:16], T.eye[:]).then_inc(S.idd, 1)
 
+    v.wait_ge(S.lds, 32)
+    for k in range(4):
+        v.tensor_copy(T.sno[32 * k:32 * k + 32, :], T.snl[0:32, :]).then_inc(S.snd, 1)
     v.wait_ge(S.ldx, 16)
     v.quantize_mx(T.xq[:], T.xp[:], T.xt[:]).then_inc(S.xqd, 1)
-    v.wait_ge(S.ldsa, 48)
-    v.wait_ge(S.ldsb, 80)
-    v.tensor_copy(T.sno[:], T.snl[:]).then_inc(S.snd, 1)
-    picks = [(k[0], len(k)) for k in groups] + [(sib, 1)]
-    v.wait_ge(S.xqd, 1)
-    v.wait_ge(S.snd, 1)
-    s.wait_ge(S.xqd, 1)
-    s.wait_ge(S.snd, 1)
-    for i, (d, n) in enumerate(picks):
-        a, b, o = CAPP * d, CAPP * (d + n), T.sno[:, 4 * d:4 * (d + n)]
-        v.tensor_copy(u32(T.slq, a, b), u32(T.xq, 0, 128).indirect(o)).then_inc(S["vp%d" % i], 1)
-        s.activation(T.slp[:, a:b], T.xp[:, 0:128].indirect(o), COPY).then_inc(S["sp%d" % i], 1)
-    a, b, o = CAPP * r, CAPP * (r + 1), T.sno[:, 4 * r:4 * r + 4]
-    v.tensor_copy(u32(T.ldq, a, b), u32(T.xq, 0, 128).indirect(o)).then_inc(S.vown, 1)
-    s.activation(T.ldp[:, a:b], T.xp[:, 0:128].indirect(o), COPY).then_inc(S.sown, 1)
+    for e in (v, s):
+        e.wait_ge(S.xqd, 1)
+        e.wait_ge(S.snd, 4)
+    picks = [[(d, 1) for d in groups[0]], [(d, 1) for d in groups[1]], [(groups[2][0], 2)], [(sib, 1)], [(r, 1)]]
 
-    needs = [[0], [1, 2, 3]]
-    nsent = 0
-    for i, codes in ((0, True), (0, False), (1, False), (1, True)):
-        for k in needs[i]:
-            g.wait_ge(S["%s%d" % ("vp" if codes else "sp", k)], 1)
+    def sides(d, n, home, land, win):
+        a = place(r, r) if d == r else at[d]
+        return (land if d == r else home)[:, a:a + CAPP * n], win, T.sno[:, 4 * d:4 * (d + n)]
+
+    out, win, o = sides(groups[0][0], 1, T.slp, T.ldp, T.xp[:, 0:128])
+    v.tensor_copy(out, win.indirect(o)).then_inc(S.sp0, 1)
+    for i, part in enumerate(picks):
+        for d, n in part:
+            out, win, o = sides(d, n, T.slq, T.ldq, u32(T.xq, 0, 128))
+            v.tensor_copy(out.bitcast(dt.uint32), win.indirect(o)).then_inc(S["vp%d" % i], 1)
+            if d != groups[0][0]:
+                out, win, o = sides(d, n, T.slp, T.ldp, T.xp[:, 0:128])
+                s.activation(out, win.indirect(o), COPY).then_inc(S["sp%d" % i], 1)
+
+    nsent = [0]
+
+    def send(parts, sem):
         tr = []
-        for d, eng in calls[i]:
+        for d, eng, src, dst in parts:
             rid, pid = topo.addr(T.cores[d], core)
-            a, c = CAPP * d, CAPP * r
-            src = u8(T.slq, a, a + CAPP) if codes else T.slp[:, a:a + CAPP]
-            dst = u8(T.ldq, c, c + CAPP) if codes else T.ldp[:, c:c + CAPP]
             tr.append(RemoteDMATransfer(dst_ids=[DstId(rid=rid, pnc=pid)], dma_engine_mask=sum(1 << e for e in eng),
-                                        remote_sem=S.arrc if codes else S.arrp, src=src, dst=dst))
-            nsent += len(eng)
+                                        remote_sem=sem, src=src, dst=dst))
+            nsent[0] += len(eng)
         g.remote_dma_fused(tr, local_sem=S.sent)
 
+    def wide(k, eng):
+        a, b = CAPP * groups[k][0], place(r, peer[k])
+        b -= at[peer[k]] - a
+        return (peer[k], eng, T.slp[:, a:a + 2 * CAPP], T.ldp[:, b:b + 2 * CAPP])
+
+    def planes(d, eng):
+        a = place(r, d)
+        return (d, eng, T.slp[:, at[d]:at[d] + CAPP], T.ldp[:, a:a + CAPP])
+
+    def codes(d, eng):
+        a = place(r, d)
+        return (d, eng, u8(T.slq, at[d], at[d] + CAPP), u8(T.ldq, a, a + CAPP))
+
+    def onward(q, eng):
+        a, b = CAPP * (FRONT - 1 if q == ends[0] else BACK + 1), place(q, sib)
+        return (sib, eng, T.ldp[:, a:a + CAPP], T.ldp[:, b:b + CAPP])
+
+    for k in range(2):
+        g.wait_ge(S["sp%d" % k], 2)
+        send([wide(k, off)], S.arrw)
+    g.wait_ge(S.sp2, 1)
+    g.wait_ge(S.sp3, 1)
+    send([planes(d, e) for d, e in deal(groups[2], off)] + [planes(sib, spare[:2])], S.arrp)
+    for k in range(3):
+        g.wait_ge(S["vp%d" % k], len(picks[k]))
+    first, last = groups[0] + other[1:], peer[1:]
+    send([codes(d, e) for d, e in deal(first, off)], S.arrc)
+    g.wait_ge(S.vp3, 1)
+    send([codes(d, e) for d, e in deal(last, off)] + [codes(sib, spare)], S.arrc)
+    g.wait_ge(S.arrw, 2 * len(off))
+    send([onward(q, e) for q, e in deal(ends, spare)], S.arrp)
+
+    s.wait_ge(S.zero, 1)
+    s.wait_ge(S.eyed, 1)
+    for t in range(4):
+        s.activation(T.idt[:, 5 * t:2048:16], T.eye[:], COPY).then_inc(S.idd, 1)
+    v.wait_ge(S.ldo, 160)
+    v.tensor_copy(T.lst[0:32, 0:32], T.sol[0:32, 3:131:4]).then_inc(S.step, 1)
+    v.wait_ge(S.step, 1)
+    v.tensor_scalar(T.blk[0:32, :], T.lst[0:32, :], 7 * CAPP, None, AluOpType.bitwise_and).then_inc(S.blkd, 1)
+    v.wait_ge(S.blkd, 1)
+    for q, t in zip(ends, (T.mvf, T.mvb)):
+        v.tensor_scalar(t[0:32, :], T.blk[0:32, :], CAPP * q, place(q, r) - CAPP * (MID + q),
+                        AluOpType.is_equal, AluOpType.mult).then_inc(S.mvd, 1)
+    v.wait_ge(S.mvd, 2)
+    v.tensor_tensor(T.mov[0:32, :], T.mvf[0:32, :], T.mvb[0:32, :], AluOpType.add).then_inc(S.movd, 1)
+    v.wait_ge(S.movd, 1)
+    v.tensor_tensor(T.col[0:32, :], T.lst[0:32, :], T.mov[0:32, :], AluOpType.add).then_inc(S.cold, 1)
+    v.wait_ge(S.cold, 1)
+    for k in range(4):
+        v.tensor_scalar(T.soo[32 * k:32 * k + 32, :], T.col[0:32, :], CAPP * (MID - FRONT), None, AluOpType.add).then_inc(S.sod, 1)
     v.wait_ge(S.idd, 4)
     v.quantize_mx(T.idq[:], T.idp[:], T.idt[:]).then_inc(S.idqd, 1)
-    v.wait_ge(S.iop, 1)
-    v.tensor_scalar(T.plow[:], T.pidx[:], 3, None, AluOpType.bitwise_and).then_inc(S.low, 1)
-    v.tensor_scalar(T.phigh[:], T.pidx[:], 15, 2, AluOpType.bitwise_and, AluOpType.arith_shift_right).then_inc(S.high, 1)
-    v.wait_ge(S.low, 1)
-    v.tensor_scalar(T.plow2[:], T.plow[:], 128, None, AluOpType.mult).then_inc(S.low2, 1)
-    v.wait_ge(S.iok, 1)
-    v.wait_ge(S.high, 1)
-    v.tensor_tensor(T.isum[:], T.phigh[:], T.kidx[:], AluOpType.add).then_inc(S.su, 1)
-    v.wait_ge(S.su, 1)
-    v.wait_ge(S.low2, 1)
-    v.tensor_tensor(T.isum2[:], T.isum[:], T.plow2[:], AluOpType.add).then_inc(S.su2, 1)
-    v.wait_ge(S.su2, 1)
-    v.tensor_copy(T.inv[:], T.isum2[:]).then_inc(S.invd, 1)
-    v.wait_ge(S.ldo2, 48)
-    v.tensor_copy(T.soo[:], T.sol[:, 3:131:4]).then_inc(S.sod, 1)
 
-    v.wait_ge(S.sod, 1)
-    v.wait_ge(S.vown, 1)
-    v.wait_ge(S.arrc, due)
-    s.wait_ge(S.sod, 1)
-    s.wait_ge(S.sown, 1)
-    s.wait_ge(S.invd, 1)
-    s.wait_ge(S.arrp, due)
+    w0, w1 = CAPP * FRONT, CAPP * (BACK + 1)
+    for e in (v, s):
+        e.wait_ge(S.sod, 4)
+        e.wait_ge(S.sp4, 1)
+        e.wait_ge(S.arrw, 2 * len(off))
+        e.wait_ge(S.arrp, len(off) + 2 + len(spare))
     for t in range(4):
-        a, b, o = 128 * t, 128 * t + 128, T.soo[:, 8 * t:8 * t + 8]
-        v.tensor_copy(u32(T.gq, a, b), u32(T.ldq, 0, 512).indirect(o)).then_inc(S["gqd%d" % t], 1)
-        s.activation(T.gp[:, a:b], T.ldp[:, 0:512].indirect(o), COPY).then_inc(S["gpd%d" % t], 1)
+        out, src = T.gp[:, 128 * t:128 * t + 128], T.ldp[:, w0:w1].indirect(T.soo[:, 8 * t:8 * t + 8])
+        (v.tensor_copy(out, src) if t in G_PLANES_ON_VECTOR else s.activation(out, src, COPY)).then_inc(S["gpd%d" % t], 1)
+    s.activation(T.fp[:, 0:512], T.ldp[:, w0:w1].indirect(T.soo[:, 32:64]), COPY).then_inc(S.fpd, 1)
+    v.wait_ge(S.vp4, 1)
+    v.wait_ge(S.arrc, 2 * len(off) + len(spare))
     for t in range(4):
-        v.wait_ge(S["gqd%d" % t], 1)
-        s.wait_ge(S["gpd%d" % t], 1)
-    v.wait_ge(S.invd, 1)
-    v.tensor_copy(u32(T.fq, 0, 512), u32(T.gq, 0, 512).indirect(T.inv[:, 0:32])).then_inc(S.fqd, 1)
-    s.activation(T.fp[:, 0:512], T.gp[:, 0:512].indirect(T.inv[:, 0:32]), COPY).then_inc(S.fpd, 1)
+        v.tensor_copy(u32(T.gq, 128 * t, 128 * t + 128),
+                      u32(T.ldq, w0, w1).indirect(T.soo[:, 8 * t:8 * t + 8])).then_inc(S["gqd%d" % t], 1)
+    v.tensor_copy(u32(T.fq, 0, 512), u32(T.ldq, w0, w1).indirect(T.soo[:, 32:64])).then_inc(S.fqd, 1)
 
     te.wait_ge(S.idqd, 1)
     for h, (a, b) in enumerate(PARTS):
@@ -223,4 +252,4 @@ def rank_program(g, core, T, topo):
             S.std2 if k < 3 else S.std, 16)
     y.wait_ge(S.std, 16 * 8)
     s.wait_ge(S.std2, 48)
-    g.wait_ge(S.sent, nsent)
+    g.wait_ge(S.sent, nsent[0])

from concourse.bass import DstId, RemoteDMATransfer
from concourse.mybir import dt, AluOpType, ActivationFunctionType

CAPP = 64
FRONT, MID, BACK = 1, 2, 10
COPY = ActivationFunctionType.Copy
PARTS = [(0, 384), (384, 512)]
ON_VECTOR = [(0, 3)]
G_PLANES_ON_VECTOR = [1, 2]

SCRATCH = {
    "xt": ("sbuf", [128, 512], "bfloat16"),
    "xq": ("sbuf", [128, 128], "float8_e4m3fn_x4"),
    "xp": ("sbuf", [128, 128], "uint8"),
    "snl": ("sbuf", [128, 32], "int32"),
    "sno": ("sbuf", [128, 32], "uint16"),
    "sol": ("sbuf", [128, 132], "int32"),
    "lst": ("sbuf", [128, 64], "int32"),
    "blk": ("sbuf", [128, 64], "int32"),
    "mvf": ("sbuf", [128, 64], "int32"),
    "mvb": ("sbuf", [128, 64], "int32"),
    "mov": ("sbuf", [128, 64], "int32"),
    "col": ("sbuf", [128, 64], "int32"),
    "soo": ("sbuf", [128, 64], "uint16"),
    "ones": ("sbuf", [128, 128], "bfloat16"),
    "eye": ("sbuf", [128, 128], "bfloat16"),
    "idt": ("sbuf", [128, 2048], "bfloat16"),
    "idq": ("sbuf", [128, 512], "float8_e4m3fn_x4"),
    "idp": ("sbuf", [128, 512], "uint8"),
    "slq": ("sbuf", [128, 512], "float8_e4m3fn_x4"),
    "slp": ("sbuf", [128, 512], "uint8"),
    "ldq": ("sbuf", [128, 768], "float8_e4m3fn_x4"),
    "ldp": ("sbuf", [128, 768], "uint8"),
    "gq": ("sbuf", [128, 512], "float8_e4m3fn_x4"),
    "gp": ("sbuf", [128, 512], "uint8"),
    "fq": ("sbuf", [128, 512], "float8_e4m3fn_x4"),
    "fp": ("sbuf", [128, 512], "uint8"),
    "bt": ("sbuf", [128, 2048], "bfloat16"),
    "bq": ("sbuf", [128, 512], "float8_e4m3fn_x4"),
    "bp": ("sbuf", [128, 512], "uint8"),
    "acc": ("psum", [128, 4096], "float32"),
}
SEMAPHORES = (["ldx", "lds", "ldo", "one", "zero", "eyed", "idd", "idqd", "snd", "step", "blkd", "mvd", "movd", "cold", "sod", "xqd",
               "fqd", "fpd", "arrw", "arrp", "arrc", "sent", "std", "std2"]
              + ["%s%d" % (a, k) for a in ("vp", "sp") for k in range(5)]
              + ["%s%d" % (a, k) for a in ("gqd", "gpd") for k in range(4)]
              + ["mm%d" % k for k in range(8)] + ["cp%d" % k for k in range(8)] + ["bqd0", "bqd1"])


def plan(r, cores, topo):
    me = cores[r]
    home = [q for q in range(len(cores)) if cores[q] in topo.cores_of(me)]
    groups = []
    for q in range(len(cores)):
        if q not in home and not any(q in k for k in groups):
            groups.append([w for w in range(len(cores)) if cores[w] in topo.cores_of(cores[q])])

    def near(k):
        return 1 if topo.mates(me, cores[k[0]]) else 2 if topo.same_plane(me, cores[k[0]]) else 0
    groups.sort(key=near)
    peer = [[q for q in k if topo.die(cores[q]) == topo.die(me)][0] for k in groups]
    other = [[q for q in k if q not in peer][0] for k in groups]
    ends = peer[:2] if r == home[1] else peer[1::-1]
    off = topo.engines(me, cores[groups[0][0]])
    spare = [e for e in topo.engines(me, [c for c in topo.cores_of(me) if c != me][0]) if e not in off]
    return {"sib": [q for q in home if q != r][0], "groups": groups, "peer": peer, "other": other, "ends": ends,
            "off": off, "spare": spare}


def deal(items, engines):
    w = len(engines) // len(items)
    return [(it, engines[w * i:w * i + w]) for i, it in enumerate(items)]


def rank_program(g, core, T, topo):
    r = T.rank_of(core)
    if r is None:
        return
    S = T.sem
    v, s, y, te = g.vector, g.scalar, g.sync, g.tensor
    P = plan(r, T.cores, topo)
    sib, groups, peer, other, ends, off, spare = [P[k] for k in ("sib", "groups", "peer", "other", "ends", "off", "spare")]

    def place(src, dst):
        e = plan(dst, T.cores, topo)["ends"]
        return CAPP * (FRONT if src == e[0] else BACK if src == e[1] else MID + src)

    at = [CAPP * d for d in range(len(T.cores))]
    at[groups[1][0]], at[groups[1][1]] = at[groups[1][1]], at[groups[1][0]]

    def u32(t, a, b):
        return t[:, a:b].bitcast(dt.uint32)

    def u8(t, a, b):
        return t[:, a:b].bitcast(dt.uint8)

    y.dma_start(T.xt[:], T.x[:]).then_inc(S.ldx, 16)
    for k in range(2):
        s.dma_start(T.snl[16 * k:16 * k + 16, :], T.sn[:]).then_inc(S.lds, 16)
    for k in range(2):
        y.dma_start(T.lst[16 * k:16 * k + 16, 32:64], T.so[:]).then_inc(S.ldo, 16)
        for u in range(4):
            a = 16 * k + 4 * u
            y.dma_start(T.sol[a:a + 4, 3 - u:131 - u], T.so[:]).then_inc(S.ldo, 16)

    g.wait_ge(S.one, 1)
    g.affine_select(T.eye[:], T.ones[:], [[-1, 128]], AluOpType.is_equal, 0.0, 0, 1).then_inc(S.eyed, 1)
    v.memset(T.ones[:], 1.0).then_inc(S.one, 1)
    v.memset(T.idt[:], 0.0).then_inc(S.zero, 1)

    v.wait_ge(S.lds, 32)
    for k in range(4):
        v.tensor_copy(T.sno[32 * k:32 * k + 32, :], T.snl[0:32, :]).then_inc(S.snd, 1)
    v.wait_ge(S.ldx, 16)
    v.quantize_mx(T.xq[:], T.xp[:], T.xt[:]).then_inc(S.xqd, 1)
    for e in (v, s):
        e.wait_ge(S.xqd, 1)
        e.wait_ge(S.snd, 4)
    picks = [[(d, 1) for d in groups[0]], [(d, 1) for d in groups[1]], [(groups[2][0], 2)], [(sib, 1)], [(r, 1)]]

    def sides(d, n, home, land, win):
        a = place(r, r) if d == r else at[d]
        return (land if d == r else home)[:, a:a + CAPP * n], win, T.sno[:, 4 * d:4 * (d + n)]

    out, win, o = sides(groups[0][0], 1, T.slp, T.ldp, T.xp[:, 0:128])
    v.tensor_copy(out, win.indirect(o)).then_inc(S.sp0, 1)
    for i, part in enumerate(picks):
        for d, n in part:
            out, win, o = sides(d, n, T.slq, T.ldq, u32(T.xq, 0, 128))
            v.tensor_copy(out.bitcast(dt.uint32), win.indirect(o)).then_inc(S["vp%d" % i], 1)
            if d != groups[0][0]:
                out, win, o = sides(d, n, T.slp, T.ldp, T.xp[:, 0:128])
                s.activation(out, win.indirect(o), COPY).then_inc(S["sp%d" % i], 1)

    nsent = [0]

    def send(parts, sem):
        tr = []
        for d, eng, src, dst in parts:
            rid, pid = topo.addr(T.cores[d], core)
            tr.append(RemoteDMATransfer(dst_ids=[DstId(rid=rid, pnc=pid)], dma_engine_mask=sum(1 << e for e in eng),
                                        remote_sem=sem, src=src, dst=dst))
            nsent[0] += len(eng)
        g.remote_dma_fused(tr, local_sem=S.sent)

    def wide(k, eng):
        a, b = CAPP * groups[k][0], place(r, peer[k])
        b -= at[peer[k]] - a
        return (peer[k], eng, T.slp[:, a:a + 2 * CAPP], T.ldp[:, b:b + 2 * CAPP])

    def planes(d, eng):
        a = place(r, d)
        return (d, eng, T.slp[:, at[d]:at[d] + CAPP], T.ldp[:, a:a + CAPP])

    def codes(d, eng):
        a = place(r, d)
        return (d, eng, u8(T.slq, at[d], at[d] + CAPP), u8(T.ldq, a, a + CAPP))

    def onward(q, eng):
        a, b = CAPP * (FRONT - 1 if q == ends[0] else BACK + 1), place(q, sib)
        return (sib, eng, T.ldp[:, a:a + CAPP], T.ldp[:, b:b + CAPP])

    for k in range(2):
        g.wait_ge(S["sp%d" % k], 2)
        send([wide(k, off)], S.arrw)
    g.wait_ge(S.sp2, 1)
    g.wait_ge(S.sp3, 1)
    send([planes(d, e) for d, e in deal(groups[2], off)] + [planes(sib, spare[:2])], S.arrp)
    for k in range(3):
        g.wait_ge(S["vp%d" % k], len(picks[k]))
    first, last = groups[0] + other[1:], peer[1:]
    send([codes(d, e) for d, e in deal(first, off)], S.arrc)
    g.wait_ge(S.vp3, 1)
    send([codes(d, e) for d, e in deal(last, off)] + [codes(sib, spare)], S.arrc)
    g.wait_ge(S.arrw, 2 * len(off))
    send([onward(q, e) for q, e in deal(ends, spare)], S.arrp)

    s.wait_ge(S.zero, 1)
    s.wait_ge(S.eyed, 1)
    for t in range(4):
        s.activation(T.idt[:, 5 * t:2048:16], T.eye[:], COPY).then_inc(S.idd, 1)
    v.wait_ge(S.ldo, 160)
    v.tensor_copy(T.lst[0:32, 0:32], T.sol[0:32, 3:131:4]).then_inc(S.step, 1)
    v.wait_ge(S.step, 1)
    v.tensor_scalar(T.blk[0:32, :], T.lst[0:32, :], 7 * CAPP, None, AluOpType.bitwise_and).then_inc(S.blkd, 1)
    v.wait_ge(S.blkd, 1)
    for q, t in zip(ends, (T.mvf, T.mvb)):
        v.tensor_scalar(t[0:32, :], T.blk[0:32, :], CAPP * q, place(q, r) - CAPP * (MID + q),
                        AluOpType.is_equal, AluOpType.mult).then_inc(S.mvd, 1)
    v.wait_ge(S.mvd, 2)
    v.tensor_tensor(T.mov[0:32, :], T.mvf[0:32, :], T.mvb[0:32, :], AluOpType.add).then_inc(S.movd, 1)
    v.wait_ge(S.movd, 1)
    v.tensor_tensor(T.col[0:32, :], T.lst[0:32, :], T.mov[0:32, :], AluOpType.add).then_inc(S.cold, 1)
    v.wait_ge(S.cold, 1)
    for k in range(4):
        v.tensor_scalar(T.soo[32 * k:32 * k + 32, :], T.col[0:32, :], CAPP * (MID - FRONT), None, AluOpType.add).then_inc(S.sod, 1)
    v.wait_ge(S.idd, 4)
    v.quantize_mx(T.idq[:], T.idp[:], T.idt[:]).then_inc(S.idqd, 1)

    w0, w1 = CAPP * FRONT, CAPP * (BACK + 1)
    for e in (v, s):
        e.wait_ge(S.sod, 4)
        e.wait_ge(S.sp4, 1)
        e.wait_ge(S.arrw, 2 * len(off))
        e.wait_ge(S.arrp, len(off) + 2 + len(spare))
    for t in range(4):
        out, src = T.gp[:, 128 * t:128 * t + 128], T.ldp[:, w0:w1].indirect(T.soo[:, 8 * t:8 * t + 8])
        (v.tensor_copy(out, src) if t in G_PLANES_ON_VECTOR else s.activation(out, src, COPY)).then_inc(S["gpd%d" % t], 1)
    s.activation(T.fp[:, 0:512], T.ldp[:, w0:w1].indirect(T.soo[:, 32:64]), COPY).then_inc(S.fpd, 1)
    v.wait_ge(S.vp4, 1)
    v.wait_ge(S.arrc, 2 * len(off) + len(spare))
    for t in range(4):
        v.tensor_copy(u32(T.gq, 128 * t, 128 * t + 128),
                      u32(T.ldq, w0, w1).indirect(T.soo[:, 8 * t:8 * t + 8])).then_inc(S["gqd%d" % t], 1)
    v.tensor_copy(u32(T.fq, 0, 512), u32(T.ldq, w0, w1).indirect(T.soo[:, 32:64])).then_inc(S.fqd, 1)

    te.wait_ge(S.idqd, 1)
    for h, (a, b) in enumerate(PARTS):
        for t in range(4):
            if h == 0:
                te.wait_ge(S["gpd%d" % t], 1)
                te.wait_ge(S["gqd%d" % t], 1)
            k = 4 * h + t
            te.matmul_mx(T.acc[:, 512 * k:512 * k + b - a], T.gq[:, 128 * t:128 * t + 128], T.gp[:, 128 * t:128 * t + 128],
                         T.idq[:, a:b], T.idp[:, a:b], True, True).then_inc(S["mm%d" % k], 1)

    for h, (a, b) in enumerate(PARTS):
        for t in range(4):
            k = 4 * h + t
            out, src = T.bt[:, 4 * a + t:4 * b:4], T.acc[:, 512 * k:512 * k + b - a]
            if (h, t) in ON_VECTOR:
                v.wait_ge(S["mm%d" % k], 1)
                v.tensor_copy(out, src).then_inc(S["cp%d" % k], 1)
            else:
                s.wait_ge(S["mm%d" % k], 1)
                s.activation(out, src, COPY).then_inc(S["cp%d" % k], 1)
        for t in range(4):
            v.wait_ge(S["cp%d" % (4 * h + t)], 1)
        v.quantize_mx(T.bq[:, a:b], T.bp[:, a:b], T.bt[:, 4 * a:4 * b]).then_inc(S["bqd%d" % h], 1)

    y.wait_ge(S.fpd, 1)
    for k in range(4):
        y.dma_start(T.fs[4 * k:4 * k + 4, 0:512], T.fp[32 * k:32 * k + 4, 0:512]).then_inc(S.std, 16)
    y.wait_ge(S.fqd, 1)
    y.dma_start(T.fc[:, :], u8(T.fq, 0, 512)).then_inc(S.std, 16)
    for h, (a, b) in enumerate(PARTS):
        y.wait_ge(S["bqd%d" % h], 1)
        y.dma_start(T.bc[:, 4 * a:4 * b], u8(T.bq, a, b)).then_inc(S.std, 16)
        s.wait_ge(S["bqd%d" % h], 1)
    for k in range(4):
        (s if k < 3 else y).dma_start(T.bs[4 * k:4 * k + 4, 0:512], T.bp[32 * k:32 * k + 4, 0:512]).then_inc(
            S.std2 if k < 3 else S.std, 16)
    y.wait_ge(S.std, 16 * 8)
    s.wait_ge(S.std2, 48)
    g.wait_ge(S.sent, nsent[0])
